import numpy as np
import ml_dtypes

BF16 = ml_dtypes.bfloat16


def bf(x):
    return np.asarray(x, np.float32).astype(BF16)


def f32(x):
    return np.asarray(x, np.float32)


def f64(x):
    return np.asarray(x).astype(np.float64)


def striped(idx):
    return np.tile(idx.reshape(-1, 16).T, (8, 1))


S, K, M, N, E, Q, V, D = 512, 128, 256, 128, 1, 128, 256, 2


def setup_inputs():
    return {"base": bf(np.random.standard_normal((M, S))), "x": bf(np.random.standard_normal((K, N))), "w": bf(1.5 * np.random.standard_normal((E, K, M)) / np.sqrt(K)), "b": f32(0.5 * np.random.standard_normal((M, 1))), "offs": striped(np.random.permutation(S)[:N])}


def reference(base, x, w, b, offs):
    idx = offs[:16].T.reshape(-1)
    z = f64(base).copy()
    for e in range(E):
        z[:, idx[e * Q : (e + 1) * Q]] += f64(w)[e].T @ f64(x)[:, e * Q : (e + 1) * Q]
    z = np.tanh(z + f64(b))
    return z.reshape(M, V, D).max(axis=2)

@@ -1,0 +1,49 @@
+import concourse.mybir as mybir
+from concourse.masks import make_identity
+
+BF16, F32, U16 = mybir.dt.bfloat16, mybir.dt.float32, mybir.dt.uint16
+TANH = mybir.ActivationFunctionType.Tanh
+MAX = mybir.AluOpType.max
+
+P = 128
+M, S, POOL = 256, 512, 2
+BLOCKS = M // P
+
+FLOPS = 2 * M * P * P + M * P
+
+
+def tile_rows_unpool_max_tanh_kernel(tc, base, x, w, b, offs, out):
+    nc = tc.nc
+    with (
+        tc.tile_pool(name="held", bufs=1) as held,
+        tc.psum_pool(name="psum", bufs=1) as psum,
+    ):
+        offsets = held.tile([P, P // 16], U16, name="offsets")
+        weights = held.tile([P, M], BF16, name="weights")
+        points = held.tile([P, P], BF16, name="points")
+        bias = held.tile([P, BLOCKS], F32, name="bias")
+        identity = held.tile([P, P], BF16, name="identity")
+        base_rows = [held.tile([P, S], BF16, name=f"base_rows{a}") for a in range(BLOCKS)]
+        windows = [psum.tile([P, S], F32, name=f"window{a}") for a in range(BLOCKS)]
+
+        for a in range(BLOCKS):
+            nc.sync.dma_start(base_rows[a][:], base[a * P : (a + 1) * P, :])
+        nc.sync.dma_start(offsets[:], offs)
+        nc.scalar.dma_start(weights[:], w[0, :, :])
+        nc.scalar.dma_start(points[:], x)
+        nc.scalar.dma_start(bias[:], b.rearrange("(a p) o -> p (a o)", p=P))
+        make_identity(nc, identity[:])
+
+        for a in range(BLOCKS):
+            nc.tensor.matmul(windows[a][:], identity[:], base_rows[a][:], start=True, stop=False)
+        for a in range(BLOCKS):
+            nc.tensor.matmul(
+                windows[a][:].indirect(offsets[:]), weights[:, a * P : (a + 1) * P], points[:], start=False, stop=True
+            )
+
+        for a in range(BLOCKS):
+            cells = held.tile([P, S], F32, name=f"cells{a}")
+            pooled = held.tile([P, S // POOL], F32, name=f"pooled{a}")
+            nc.scalar.activation(cells[:], windows[a][:], TANH, bias=bias[:, a : a + 1])
+            nc.vector.tensor_tensor(pooled[:], cells[:, 0::2], cells[:, 1::2], MAX)
+            nc.sync.dma_start(out[a * P : (a + 1) * P, :], pooled[:])

@@ -29,10 +29,15 @@ def tile_rows_unpool_max_tanh_kernel(tc, base, x, w, b, offs, out):
         for a in range(BLOCKS):
             nc.sync.dma_start(base_rows[a][:], base[a * P : (a + 1) * P, :])
         nc.sync.dma_start(offsets[:], offs)
+
         nc.scalar.dma_start(weights[:], w[0, :, :])
         nc.scalar.dma_start(points[:], x)
         nc.scalar.dma_start(bias[:], b.rearrange("(a p) o -> p (a o)", p=P))
         make_identity(nc, identity[:])
+
+        scratch = held.tile([P, 1], F32, name="scratch")
+        nc.vector.memset(scratch[:], 0.0)
+        nc.scalar.activation(scratch[:], scratch[:], TANH)
 
         for a in range(BLOCKS):
             nc.tensor.matmul(windows[a][:], identity[:], base_rows[a][:], start=True, stop=False)
@@ -41,9 +46,16 @@ def tile_rows_unpool_max_tanh_kernel(tc, base, x, w, b, offs, out):
                 windows[a][:].indirect(offsets[:]), weights[:, a * P : (a + 1) * P], points[:], start=False, stop=True
             )
 
-        for a in range(BLOCKS):
-            cells = held.tile([P, S], F32, name=f"cells{a}")
-            pooled = held.tile([P, S // POOL], F32, name=f"pooled{a}")
-            nc.scalar.activation(cells[:], windows[a][:], TANH, bias=bias[:, a : a + 1])
-            nc.vector.tensor_tensor(pooled[:], cells[:, 0::2], cells[:, 1::2], MAX)
-            nc.sync.dma_start(out[a * P : (a + 1) * P, :], pooled[:])
+        cells = held.tile([P, S], F32, name="cells")
+        pooled = held.tile([P, S // POOL], F32, name="pooled")
+        nc.scalar.activation(cells[:], windows[0][:], TANH, bias=bias[:, 0:1])
+        nc.vector.tensor_tensor(pooled[:], cells[:, 0::2], cells[:, 1::2], MAX)
+        nc.sync.dma_start(out[0:P, :], pooled[:])
+
+        largest = held.tile([P, S // POOL], F32, name="largest")
+        squashed = held.tile([P, S // POOL], F32, name="squashed")
+        nc.vector.tensor_reduce(
+            largest[:], windows[1][:].rearrange("p (v d) -> p v d", d=POOL), mybir.AxisListType.X, MAX
+        )
+        nc.scalar.activation(squashed[:], largest[:], TANH, bias=bias[:, 1:2])
+        nc.scalar.dma_start(out[P:M, :], squashed[:])

import concourse.mybir as mybir
from concourse.masks import make_identity

BF16, F32, U16 = mybir.dt.bfloat16, mybir.dt.float32, mybir.dt.uint16
TANH = mybir.ActivationFunctionType.Tanh
MAX = mybir.AluOpType.max

P = 128
M, S, POOL = 256, 512, 2
BLOCKS = M // P

FLOPS = 2 * M * P * P + M * P


def tile_rows_unpool_max_tanh_kernel(tc, base, x, w, b, offs, out):
    nc = tc.nc
    with (
        tc.tile_pool(name="held", bufs=1) as held,
        tc.psum_pool(name="psum", bufs=1) as psum,
    ):
        offsets = held.tile([P, P // 16], U16, name="offsets")
        weights = held.tile([P, M], BF16, name="weights")
        points = held.tile([P, P], BF16, name="points")
        bias = held.tile([P, BLOCKS], F32, name="bias")
        identity = held.tile([P, P], BF16, name="identity")
        base_rows = [held.tile([P, S], BF16, name=f"base_rows{a}") for a in range(BLOCKS)]
        windows = [psum.tile([P, S], F32, name=f"window{a}") for a in range(BLOCKS)]

        for a in range(BLOCKS):
            nc.sync.dma_start(base_rows[a][:], base[a * P : (a + 1) * P, :])
        nc.sync.dma_start(offsets[:], offs)

        nc.scalar.dma_start(weights[:], w[0, :, :])
        nc.scalar.dma_start(points[:], x)
        nc.scalar.dma_start(bias[:], b.rearrange("(a p) o -> p (a o)", p=P))
        make_identity(nc, identity[:])

        scratch = held.tile([P, 1], F32, name="scratch")
        nc.vector.memset(scratch[:], 0.0)
        nc.scalar.activation(scratch[:], scratch[:], TANH)

        for a in range(BLOCKS):
            nc.tensor.matmul(windows[a][:], identity[:], base_rows[a][:], start=True, stop=False)
        for a in range(BLOCKS):
            nc.tensor.matmul(
                windows[a][:].indirect(offsets[:]), weights[:, a * P : (a + 1) * P], points[:], start=False, stop=True
            )

        cells = held.tile([P, S], F32, name="cells")
        pooled = held.tile([P, S // POOL], F32, name="pooled")
        nc.scalar.activation(cells[:], windows[0][:], TANH, bias=bias[:, 0:1])
        nc.vector.tensor_tensor(pooled[:], cells[:, 0::2], cells[:, 1::2], MAX)
        nc.sync.dma_start(out[0:P, :], pooled[:])

        largest = held.tile([P, S // POOL], F32, name="largest")
        squashed = held.tile([P, S // POOL], F32, name="squashed")
        nc.vector.tensor_reduce(
            largest[:], windows[1][:].rearrange("p (v d) -> p v d", d=POOL), mybir.AxisListType.X, MAX
        )
        nc.scalar.activation(squashed[:], largest[:], TANH, bias=bias[:, 1:2])
        nc.scalar.dma_start(out[P:M, :], squashed[:])
